import numpy as np
import ml_dtypes


def mxq(x, axis, fmt="e4m3"):
    dtype, down = {"e4m3": (ml_dtypes.float8_e4m3fn, 7), "e5m2": (ml_dtypes.float8_e5m2, 14)}[fmt]
    v = np.moveaxis(np.asarray(x, np.float32).astype(ml_dtypes.bfloat16).astype(np.float64), axis, -1)
    blocks = v.reshape(v.shape[:-1] + (-1, 32))
    amax = np.abs(blocks).max(-1, keepdims=True)
    byte = np.maximum(np.where(amax > 0, np.frexp(amax)[1] - 1 + 127, 0) - down, 1)
    scale = np.exp2(byte - 127.0)
    codes = (blocks / scale).astype(np.float32).astype(dtype).astype(np.float64)
    return np.moveaxis((codes * scale).reshape(v.shape), -1, axis)


WIDE = False


def mx_kscale(k):
    if not WIDE:
        return np.ones(k)
    levels = np.array([10, -10, 5, -5, 0])
    if k % 512:
        return np.exp2(np.random.permutation(np.resize(levels, k // 32))).repeat(32)
    a = np.empty((k // 512, 16))
    for p in range(k // 512):
        a[p, :8] = np.random.permutation(np.resize(levels, 8))
        for g in range(8):
            far = levels[np.abs(levels - a[p, g]) >= 10]
            a[p, g + 8] = far[np.random.randint(len(far))]
    return np.exp2(a.ravel()).repeat(32)


def f64(x):
    return np.asarray(x).astype(np.float64)


def striped(idx):
    return np.tile(idx.reshape(-1, 16).T, (8, 1)).astype(np.uint16)


def unstriped(offs):
    return offs[:16].T.reshape(-1).astype(np.int64)


E2M1 = np.array([0.0, 0.5, 1.0, 1.5, 2.0, 3.0, 4.0, 6.0, -0.0, -0.5, -1.0, -1.5, -2.0, -3.0, -4.0, -6.0])


def pack_weight(w, fmt):
    k, n = w.shape
    w = f64(np.asarray(w, np.float32).astype(ml_dtypes.bfloat16)).reshape(k // 32, 32, n)
    amax = np.abs(w).max(1)
    if fmt == "e4m3":
        byte = np.frexp(amax)[1] - 1 + 127 - 7
    else:
        mant, ex = np.frexp(amax / 6.0)
        byte = np.where(mant > 0.5, ex, ex - 1) + 127
    byte = np.clip(np.where(amax > 0, byte, 1), 1, 254)
    scaled = (w * np.exp2(127.0 - byte)[:, None, :]).reshape(k, n).astype(np.float32)
    by_word = np.ascontiguousarray(scaled.reshape(k // 512, 128, 4, n).transpose(0, 1, 3, 2))
    if fmt == "e4m3":
        words = by_word.astype(ml_dtypes.float8_e4m3fn).view(np.uint8)
    else:
        c = by_word.astype(ml_dtypes.float4_e2m1fn).view(np.uint8) & 0xF
        words = (c[..., 0::2] | (c[..., 1::2] << 4)).reshape(k // 512, 128, 2 * n)
    return np.ascontiguousarray(words), np.ascontiguousarray(byte.astype(np.uint8).reshape(k // 512, 16, n))


def unpack_weight(words, scales, fmt):
    g, _, n = scales.shape
    words = np.ascontiguousarray(words).reshape(g, 128, n, -1)
    if fmt == "e4m3":
        vals = words.view(ml_dtypes.float8_e4m3fn).astype(np.float64)
    else:
        nib = np.empty((g, 128, n, 4), np.uint8)
        nib[..., 0::2] = words & 0xF
        nib[..., 1::2] = words >> 4
        vals = E2M1[nib]
    vals = vals * np.repeat(np.exp2(scales.astype(np.float64) - 127.0), 8, axis=1)[..., None]
    return vals.transpose(0, 1, 3, 2).reshape(g * 512, n)


def gelu(v):
    return 0.5 * v * (1.0 + np.tanh(np.sqrt(2.0 / np.pi) * (v + 0.044715 * v**3)))


K, K2, H, N, T, S, P, T2 = 1024, 512, 1024, 512, 2048, 1024, 512, 2048

def setup_inputs():
    n = np.random.standard_normal
    s, s2, u = mx_kscale(K)[:, None], mx_kscale(K2)[:, None], mx_kscale(H)[:, None]
    tab_words, tab_scales = pack_weight(n((K, T)) * s, "e4m3")
    tab2_words, tab2_scales = pack_weight(n((K2, T)) * s2, "e4m3")
    w2_words, w2_scales = pack_weight(0.3 * n((K2, H)) / np.sqrt(K2) / s2, "e2m1")
    w4_words, w4_scales = pack_weight(1.2 * n((H, N)) / np.sqrt(H) / u, "e2m1")
    perm = np.random.permutation(T2)
    return {
        "tab_words": tab_words, "tab_scales": tab_scales,
        "tab2_words": tab2_words, "tab2_scales": tab2_scales,
        "offs": striped(np.random.permutation(T)[:S]), "offs2": striped(np.random.permutation(T)[:P]),
        "pos1": striped(np.random.permutation(S)[:P]),
        "offs3": striped(perm[:S]), "offs4": striped(perm[S:S + P]),
        "w1": (1.1 * n((K, H)) / np.sqrt(K) / s * u.T).astype(np.float32),
        "r1": (np.exp(0.3 * n(H)) / u[:, 0]).astype(np.float32),
        "w2_words": w2_words, "w2_scales": w2_scales,
        "w3": (0.54 * n((K2, H)) / np.sqrt(K2) / s2).astype(np.float32),
        "w4_words": w4_words, "w4_scales": w4_scales,
        "w5": (3.0 * n((H, N)) / np.sqrt(H) / u).astype(np.float32),
        "w6": (0.9 * n((K2, N)) / np.sqrt(K2) / s2).astype(np.float32),
        "page1": n((N, T2)).astype(np.float32),
        "wg1": np.exp(0.3 * n((128, S))).astype(np.float32), "wg2": np.exp(0.3 * n((128, P))).astype(np.float32)}

def reference(tab_words, tab_scales, tab2_words, tab2_scales, offs, offs2, pos1, offs3, offs4, w1, r1,
              w2_words, w2_scales, w3, w4_words, w4_scales, w5, w6, page1, wg1, wg2):
    v = unpack_weight(tab_words, tab_scales, "e4m3")[:, unstriped(offs)]
    v2 = unpack_weight(tab2_words, tab2_scales, "e4m3")[:, unstriped(offs2)]
    h1 = mxq(f64(w1), 0, "e4m3").T @ v
    d1 = f64(r1)[:, None] * h1
    z1 = 0.5 * h1 * (1.0 + np.tanh(0.7978845608 * (d1 + 0.044715 * d1 ** 3)))
    h2 = (unpack_weight(w2_words, w2_scales, "e2m1").T @ v2) + np.sin(mxq(f64(w3), 0, "e4m3").T @ v2)
    z2 = h2 * h1[:, unstriped(pos1)]
    y1 = unpack_weight(w4_words, w4_scales, "e2m1").T @ mxq(z1, 0, "e4m3")
    y2 = mxq(f64(w5), 0, "e4m3").T @ mxq(z2, 0, "e4m3") + mxq(f64(w6), 0, "e4m3").T @ v2
    out = f64(page1).copy()
    out[:, unstriped(offs3)] = np.tile(f64(wg1), (N // 128, 1)) * y1
    out[:, unstriped(offs4)] = np.tile(f64(wg2), (N // 128, 1)) * y2
    return out

@@ -1,0 +1,286 @@
+import math
+from contextlib import ExitStack
+
+import concourse.mybir as mybir
+
+K, K2, H, N, T, S, C, T2 = 1024, 512, 1024, 512, 2048, 1024, 512, 2048
+FLOPS = 2 * (K * H * S + 2 * K2 * H * C + H * N * S + H * N * C + K2 * N * C)
+
+F32 = mybir.dt.float32
+BF16 = mybir.dt.bfloat16
+I32 = mybir.dt.int32
+U32 = mybir.dt.uint32
+U16 = mybir.dt.uint16
+U8 = mybir.dt.uint8
+FP8X4 = mybir.dt.float8_e4m3fn_x4
+FP4X4 = mybir.dt.float4_e2m1fn_x4
+ALU = mybir.AluOpType
+ACT = mybir.ActivationFunctionType
+
+P = 128
+PACK = 4
+PASS = P * PACK
+CHUNK = 512
+LIST_COLS = CHUNK // 16
+ROUND_TO_INTEGER = 1.5 * 2.0**23
+
+
+def tile_list_pallet_pool_features_kernel(
+    tc, tab_words, tab_scales, tab2_words, tab2_scales, offs, offs2, pos1, offs3, offs4, w1, r1,
+    w2_words, w2_scales, w3, w4_words, w4_scales, w5, w6, page1, wg1, wg2, out,
+):
+    nc = tc.nc
+    with ExitStack() as ctx:
+        keep = ctx.enter_context(tc.tile_pool(name="keep", bufs=1))
+        ring = ctx.enter_context(tc.tile_pool(name="ring", bufs=2))
+        psum = ctx.enter_context(tc.psum_pool(name="psum", bufs=1))
+
+        def held(name, shape, dtype):
+            return keep.tile(shape, dtype, name=name, align_bytes=64)
+
+        def load(name, source, dtype):
+            tile = held(name, list(source.shape), dtype)
+            nc.sync.dma_start(tile[:], source)
+            return tile
+
+        def zeroed_plane(name, columns):
+            plane = held(name, [P, columns], U8)
+            nc.vector.memset(plane[:].bitcast(I32), 0)
+            return plane
+
+        def load_words(name, words):
+            return load(name, words.rearrange("p t i -> p (t i)").bitcast(I32), I32)
+
+        def load_weight(weight, a, b):
+            raw = ring.tile([P, PACK, CHUNK], F32, name="raw", bufs=3)
+            rows = weight[a * PASS : (a + 1) * PASS, b * CHUNK : (b + 1) * CHUNK]
+            nc.sync.dma_start(raw[:], rows.rearrange("(p j) c -> p j c", j=PACK))
+            return raw
+
+        def copy_on(engine, dst, src):
+            if engine == "vector":
+                nc.vector.tensor_copy(dst, src)
+            else:
+                nc.scalar.copy(dst, src)
+
+        def grouped_tile():
+            return ring.tile([P, CHUNK * PACK], BF16, name="grouped", bufs=4, align_bytes=64)
+
+        def quantize(name, grouped):
+            codes = held(name + "_codes", [P, CHUNK], U32)
+            scales = held(name + "_scales", [P, CHUNK], U8)
+            nc.vector.quantize_mx(out=codes[:].bitcast(FP8X4), scales=scales[:], in_=grouped[:])
+            return codes[:].bitcast(FP8X4), scales[:]
+
+        def word_order(grouped):
+            return grouped[:].rearrange("p (c i j) -> p c j i", i=4, j=PACK)
+
+        def plane_order(planes):
+            return planes[:].rearrange("p j (c i) -> p c j i", i=4)
+
+        def quantize_dealt(name, raw, engine):
+            grouped = grouped_tile()
+            copy_on(
+                engine,
+                grouped[:].rearrange("p (t m j) -> p m j t", t=PACK, j=PACK),
+                raw[:].rearrange("p j (m t) -> p m j t", t=PACK),
+            )
+            return quantize(name, grouped)
+
+        def quantize_plain(name, raw, engine):
+            grouped = grouped_tile()
+            copy_on(engine, word_order(grouped), plane_order(raw))
+            return quantize(name, grouped)
+
+        def gather(name, window, offsets, dtype):
+            picked = held(name, [P, CHUNK], dtype)
+            nc.vector.tensor_copy(picked[:], window[:].bitcast(dtype).indirect(offsets))
+            return picked
+
+        def columns(operand, i):
+            codes, scales = operand
+            return codes[:, i * P : (i + 1) * P], scales[:, i * P : (i + 1) * P]
+
+        def product(passes):
+            bank = psum.tile([P, CHUNK], F32, name="bank", bufs=8)
+            for i, (stationary, moving) in enumerate(passes):
+                nc.tensor.matmul_mx(
+                    out=bank[:], lhsT=stationary[0], lhsT_scale=stationary[1], rhs=moving[0], rhs_scale=moving[1],
+                    start=(i == 0), stop=(i == len(passes) - 1),
+                )
+            return bank
+
+        tab_plane = zeroed_plane("tab_plane", T)
+        tab2_plane = zeroed_plane("tab2_plane", T)
+        w4_plane = zeroed_plane("w4_plane", 2 * N)
+        w2_plane = zeroed_plane("w2_plane", H)
+
+        idx = load("idx", offs, U16)
+        tab = [load_words("tab_0", tab_words[0])]
+        for q in range(4):
+            nc.sync.dma_start(tab_plane[32 * q : 32 * q + 8, :].bitcast(I32), tab_scales[:, 4 * q : 4 * q + 4, :].bitcast(I32))
+        w1_raw = {(0, 0): load_weight(w1, 0, 0)}
+        tab.append(load_words("tab_1", tab_words[1]))
+        w1_raw[(1, 0)] = load_weight(w1, 1, 0)
+        slope = load("slope", r1.rearrange("(b p t) -> p b t", p=P, t=PACK), F32)
+        w1_raw[(0, 1)] = load_weight(w1, 0, 1)
+        w1_raw[(1, 1)] = load_weight(w1, 1, 1)
+        idx2 = load("idx2", offs2, U16)
+        tab2 = load_words("tab2", tab2_words[0])
+        for q in range(4):
+            nc.sync.dma_start(tab2_plane[32 * q : 32 * q + 4, :].bitcast(I32), tab2_scales[0, 4 * q : 4 * q + 4, :].bitcast(I32))
+        w4_codes = load("w4_codes", w4_words.rearrange("a p c -> p a c").bitcast(I32), I32)
+        for q in range(4):
+            nc.sync.dma_start(
+                w4_plane[32 * q : 32 * q + 4, :].bitcast(I32).rearrange("r (a c) -> r a c", a=2),
+                w4_scales[:, 4 * q : 4 * q + 4, :].bitcast(I32).rearrange("a r c -> r a c"),
+            )
+        idx3 = load("idx3", offs3, U16)
+        gain1 = load("gain1", wg1, F32)
+
+        def load_page(n):
+            return load("page_%d" % n, page1[n * P : (n + 1) * P, :], F32)
+
+        pages = [load_page(0), load_page(1)]
+        w3_raw = [load_weight(w3, 0, 0)]
+        w2_raw = load("w2_raw", w2_words[0].bitcast(I32), I32)
+        for q in range(4):
+            nc.sync.dma_start(w2_plane[32 * q : 32 * q + 4, :].bitcast(I32), w2_scales[0, 4 * q : 4 * q + 4, :].bitcast(I32))
+        home = load("home", pos1, U16)
+        pages.append(load_page(2))
+
+        def chunk_offsets(offsets, c):
+            return offsets[:, c * LIST_COLS : (c + 1) * LIST_COLS]
+
+        v_words, v_plane, w1_mx = {}, {}, {}
+        for c in range(2):
+            v_words[(0, c)] = gather("v_0_%d" % c, tab[0], chunk_offsets(idx, c), U32)
+            v_plane[c] = gather("v_plane_%d" % c, tab_plane, chunk_offsets(idx, c), U8)
+        w1_mx[(0, 0)] = quantize_dealt("w1_0_0", w1_raw[(0, 0)], "scalar")
+        for c in range(2):
+            v_words[(1, c)] = gather("v_1_%d" % c, tab[1], chunk_offsets(idx, c), U32)
+        v = [[(v_words[(a, c)][:].bitcast(FP8X4), v_plane[c][4 * a :, :]) for a in range(2)] for c in range(2)]
+        w1_mx[(1, 0)] = quantize_dealt("w1_1_0", w1_raw[(1, 0)], "vector")
+        inverse = held("inverse", [P, 2, PACK], F32)
+        nc.vector.reciprocal(inverse[:], slope[:])
+        for a in range(2):
+            w1_mx[(a, 1)] = quantize_dealt("w1_%d_1" % a, w1_raw[(a, 1)], "vector")
+
+        w3_raw.append(load_weight(w3, 0, 1))
+        pages.append(load_page(3))
+        idx4 = load("idx4", offs4, U16)
+        gain2 = load("gain2", wg2, F32)
+
+        h1 = {}
+        for b in range(2):
+            for t in range(PACK):
+                h1[(b, t)] = held("h1_%d_%d" % (b, t), [P, S], F32)
+
+        def planes_tile():
+            return ring.tile([P, PACK, CHUNK], F32, name="planes", bufs=2)
+
+        def depots(c, b):
+            gelu = planes_tile()
+            banks = []
+            for t in range(PACK):
+                bank = product([(columns(w1_mx[(a, b)], t), v[c][a]) for a in range(2)])
+                nc.scalar.activation(gelu[:, t, :], bank[:], ACT.Gelu_apprx_tanh, scale=slope[:, b, t : t + 1])
+                banks.append(bank)
+            grouped = grouped_tile()
+            factor = inverse[:, b, :].unsqueeze(1).unsqueeze(3).to_broadcast([P, CHUNK // 4, PACK, 4])
+            nc.vector.tensor_tensor(word_order(grouped), plane_order(gelu), factor, ALU.mult)
+            return quantize("z1_%d_%d" % (c, b), grouped), banks
+
+        def keep_h1(c, b, banks):
+            for t in range(PACK):
+                nc.scalar.copy(h1[(b, t)][:, c * CHUNK : (c + 1) * CHUNK], banks[t][:])
+
+        def place(n, passes, offsets, gain):
+            bank = product(passes)
+            y = ring.tile([P, CHUNK], F32, name="y", bufs=3)
+            nc.scalar.copy(y[:], bank[:])
+            nc.vector.tensor_tensor(pages[n][:].indirect(offsets), y[:], gain, ALU.mult)
+
+        w4_bytes = w4_codes[:].bitcast(U8)
+
+        def w4_columns(b, n):
+            codes = w4_bytes[:, b, 2 * n * P : 2 * (n + 1) * P].bitcast(FP4X4)
+            return codes, w4_plane[:, b * N + n * P : b * N + (n + 1) * P]
+
+        z1 = {}
+
+        def place_depots(c, n):
+            passes = [(w4_columns(b, n), z1[(c, b)]) for b in range(2)]
+            place(n, passes, chunk_offsets(idx3, c), gain1[:, c * CHUNK : (c + 1) * CHUNK])
+
+        for b in range(2):
+            z1[(0, b)], banks = depots(0, b)
+            keep_h1(0, b, banks)
+        v2_words = gather("v2", tab2, idx2[:], U32)
+        v2_plane = gather("v2_plane", tab2_plane, idx2[:], U8)
+        v2 = (v2_words[:].bitcast(FP8X4), v2_plane[:])
+
+        place_depots(0, 0)
+        place_depots(0, 1)
+        z1[(1, 0)], banks = depots(1, 0)
+        w3_mx = [quantize_dealt("w3_0", w3_raw[0], "scalar")]
+        keep_h1(1, 0, banks)
+        z1[(1, 1)], last_banks = depots(1, 1)
+
+        w2_dealt = held("w2_dealt", [P, H], U16)
+        nc.vector.tensor_copy(
+            w2_dealt[:].rearrange("p (b t m) -> p b m t", b=2, t=PACK),
+            w2_raw[:].bitcast(U16).rearrange("p (b m t) -> p b m t", b=2, t=PACK),
+        )
+        w2_dealt_plane = held("w2_dealt_plane", [P, H], U8)
+        nc.vector.tensor_copy(
+            w2_dealt_plane[:].rearrange("p (b t m) -> p b m t", b=2, t=PACK),
+            w2_plane[:].rearrange("p (b m t) -> p b m t", b=2, t=PACK),
+        )
+        w5_raw = [load_weight(w5, a, 0) for a in range(2)]
+        w6_raw = load_weight(w6, 0, 0)
+
+        def reduce_angle(b, t):
+            angle = product([(columns(w3_mx[b], t), v2)])
+            shifted = ring.tile([P, CHUNK], U32, name="shifted", bufs=2)
+            nc.scalar.activation(shifted[:], angle[:], ACT.Copy, bias=ROUND_TO_INTEGER, scale=1.0 / (2.0 * math.pi))
+            h2 = ring.tile([P, CHUNK], F32, name="h2", bufs=4)
+            nc.scalar.activation(h2[:], shifted[:], ACT.Copy, bias=-ROUND_TO_INTEGER, scale=1.0)
+            nc.vector.scalar_tensor_tensor(h2[:], h2[:], -2.0 * math.pi, angle[:], ALU.mult, ALU.add)
+            return h2
+
+        def meet_depot(b, t, h2, planes):
+            i = b * PACK + t
+            nc.scalar.activation(h2[:], h2[:], ACT.Sin)
+            w2_columns = (w2_dealt[:, i * P : (i + 1) * P].bitcast(FP4X4), w2_dealt_plane[:, i * P : (i + 1) * P])
+            linear = product([(w2_columns, v2)])
+            nc.vector.tensor_tensor(h2[:], linear[:], h2[:], ALU.add)
+            nc.vector.tensor_tensor(planes[:, t, :], h1[(b, t)][:].indirect(home[:]), h2[:], ALU.mult)
+
+        def customers(b, pair, planes, c, n):
+            slots = (2 * pair, 2 * pair + 1)
+            angles = [reduce_angle(b, t) for t in slots]
+            place_depots(c, n)
+            for t, h2 in zip(slots, angles):
+                meet_depot(b, t, h2, planes)
+
+        planes = [planes_tile()]
+        customers(0, 0, planes[0], 0, 2)
+        w3_mx.append(quantize_dealt("w3_1", w3_raw[1], "scalar"))
+        customers(0, 1, planes[0], 0, 3)
+        keep_h1(1, 1, last_banks)
+        w5_mx = [quantize_plain("w5_0", w5_raw[0], "scalar")]
+        planes.append(planes_tile())
+        customers(1, 0, planes[1], 1, 0)
+        z2 = [quantize_plain("z2_0", planes[0], "scalar")]
+        w5_mx.append(quantize_plain("w5_1", w5_raw[1], "scalar"))
+        customers(1, 1, planes[1], 1, 1)
+        w6_mx = quantize_plain("w6", w6_raw, "scalar")
+        place_depots(1, 2)
+        z2.append(quantize_plain("z2_1", planes[1], "scalar"))
+        place_depots(1, 3)
+
+        for n in range(N // P):
+            passes = [(columns(w6_mx, n), v2)] + [(columns(w5_mx[b], n), z2[b]) for b in range(2)]
+            place(n, passes, idx4[:], gain2[:])
+            nc.sync.dma_start(out[n * P : (n + 1) * P, :], pages[n][:])

@@ -52,7 +52,7 @@ def tile_list_pallet_pool_features_kernel(
             return load(name, words.rearrange("p t i -> p (t i)").bitcast(I32), I32)
 
         def load_weight(weight, a, b):
-            raw = ring.tile([P, PACK, CHUNK], F32, name="raw", bufs=3)
+            raw = ring.tile([P, PACK, CHUNK], F32, name="raw", bufs=4)
             rows = weight[a * PASS : (a + 1) * PASS, b * CHUNK : (b + 1) * CHUNK]
             nc.sync.dma_start(raw[:], rows.rearrange("(p j) c -> p j c", j=PACK))
             return raw
@@ -64,7 +64,7 @@ def tile_list_pallet_pool_features_kernel(
                 nc.scalar.copy(dst, src)
 
         def grouped_tile():
-            return ring.tile([P, CHUNK * PACK], BF16, name="grouped", bufs=4, align_bytes=64)
+            return ring.tile([P, CHUNK * PACK], BF16, name="grouped", bufs=3, align_bytes=64)
 
         def quantize(name, grouped):
             codes = held(name + "_codes", [P, CHUNK], U32)
@@ -115,20 +115,25 @@ def tile_list_pallet_pool_features_kernel(
         w4_plane = zeroed_plane("w4_plane", 2 * N)
         w2_plane = zeroed_plane("w2_plane", H)
 
+        def load_page(n):
+            return load("page_%d" % n, page1[n * P : (n + 1) * P, :], F32)
+
+        w1_raw, pages = {}, []
         idx = load("idx", offs, U16)
         tab = [load_words("tab_0", tab_words[0])]
         for q in range(4):
             nc.sync.dma_start(tab_plane[32 * q : 32 * q + 8, :].bitcast(I32), tab_scales[:, 4 * q : 4 * q + 4, :].bitcast(I32))
-        w1_raw = {(0, 0): load_weight(w1, 0, 0)}
+        w1_raw[(0, 0)] = load_weight(w1, 0, 0)
         tab.append(load_words("tab_1", tab_words[1]))
         w1_raw[(1, 0)] = load_weight(w1, 1, 0)
-        slope = load("slope", r1.rearrange("(b p t) -> p b t", p=P, t=PACK), F32)
         w1_raw[(0, 1)] = load_weight(w1, 0, 1)
         w1_raw[(1, 1)] = load_weight(w1, 1, 1)
+        slope = load("slope", r1.rearrange("(b p t) -> p b t", p=P, t=PACK), F32)
         idx2 = load("idx2", offs2, U16)
         tab2 = load_words("tab2", tab2_words[0])
         for q in range(4):
             nc.sync.dma_start(tab2_plane[32 * q : 32 * q + 4, :].bitcast(I32), tab2_scales[0, 4 * q : 4 * q + 4, :].bitcast(I32))
+        w3_raw = [load_weight(w3, 0, 0)]
         w4_codes = load("w4_codes", w4_words.rearrange("a p c -> p a c").bitcast(I32), I32)
         for q in range(4):
             nc.sync.dma_start(
@@ -137,12 +142,8 @@ def tile_list_pallet_pool_features_kernel(
             )
         idx3 = load("idx3", offs3, U16)
         gain1 = load("gain1", wg1, F32)
-
-        def load_page(n):
-            return load("page_%d" % n, page1[n * P : (n + 1) * P, :], F32)
-
-        pages = [load_page(0), load_page(1)]
-        w3_raw = [load_weight(w3, 0, 0)]
+        pages.append(load_page(0))
+        pages.append(load_page(1))
         w2_raw = load("w2_raw", w2_words[0].bitcast(I32), I32)
         for q in range(4):
             nc.sync.dma_start(w2_plane[32 * q : 32 * q + 4, :].bitcast(I32), w2_scales[0, 4 * q : 4 * q + 4, :].bitcast(I32))
@@ -179,13 +180,17 @@ def tile_list_pallet_pool_features_kernel(
         def planes_tile():
             return ring.tile([P, PACK, CHUNK], F32, name="planes", bufs=2)
 
-        def depots(c, b):
+        def depots(c, b, engine="fused"):
             gelu = planes_tile()
             banks = []
             for t in range(PACK):
                 bank = product([(columns(w1_mx[(a, b)], t), v[c][a]) for a in range(2)])
                 nc.scalar.activation(gelu[:, t, :], bank[:], ACT.Gelu_apprx_tanh, scale=slope[:, b, t : t + 1])
                 banks.append(bank)
+            if engine != "fused":
+                for t in range(PACK):
+                    nc.scalar.activation(gelu[:, t, :], gelu[:, t, :], ACT.Copy, scale=inverse[:, b, t : t + 1])
+                return quantize_plain("z1_%d_%d" % (c, b), gelu, engine), banks
             grouped = grouped_tile()
             factor = inverse[:, b, :].unsqueeze(1).unsqueeze(3).to_broadcast([P, CHUNK // 4, PACK, 4])
             nc.vector.tensor_tensor(word_order(grouped), plane_order(gelu), factor, ALU.mult)
@@ -220,12 +225,12 @@ def tile_list_pallet_pool_features_kernel(
         v2_plane = gather("v2_plane", tab2_plane, idx2[:], U8)
         v2 = (v2_words[:].bitcast(FP8X4), v2_plane[:])
 
+        z1[(1, 0)], banks = depots(1, 0)
         place_depots(0, 0)
         place_depots(0, 1)
-        z1[(1, 0)], banks = depots(1, 0)
         w3_mx = [quantize_dealt("w3_0", w3_raw[0], "scalar")]
         keep_h1(1, 0, banks)
-        z1[(1, 1)], last_banks = depots(1, 1)
+        z1[(1, 1)], last_banks = depots(1, 1, "vector")
 
         w2_dealt = held("w2_dealt", [P, H], U16)
         nc.vector.tensor_copy(

@@ -127,6 +127,9 @@ def tile_list_pallet_pool_features_kernel(
         tab.append(load_words("tab_1", tab_words[1]))
         w1_raw[(1, 0)] = load_weight(w1, 1, 0)
         w1_raw[(0, 1)] = load_weight(w1, 0, 1)
+        w2_raw = load("w2_raw", w2_words[0].bitcast(I32), I32)
+        for q in range(4):
+            nc.sync.dma_start(w2_plane[32 * q : 32 * q + 4, :].bitcast(I32), w2_scales[0, 4 * q : 4 * q + 4, :].bitcast(I32))
         w1_raw[(1, 1)] = load_weight(w1, 1, 1)
         slope = load("slope", r1.rearrange("(b p t) -> p b t", p=P, t=PACK), F32)
         idx2 = load("idx2", offs2, U16)
@@ -144,9 +147,6 @@ def tile_list_pallet_pool_features_kernel(
         gain1 = load("gain1", wg1, F32)
         pages.append(load_page(0))
         pages.append(load_page(1))
-        w2_raw = load("w2_raw", w2_words[0].bitcast(I32), I32)
-        for q in range(4):
-            nc.sync.dma_start(w2_plane[32 * q : 32 * q + 4, :].bitcast(I32), w2_scales[0, 4 * q : 4 * q + 4, :].bitcast(I32))
         home = load("home", pos1, U16)
         pages.append(load_page(2))
 
@@ -169,8 +169,6 @@ def tile_list_pallet_pool_features_kernel(
 
         w3_raw.append(load_weight(w3, 0, 1))
         pages.append(load_page(3))
-        idx4 = load("idx4", offs4, U16)
-        gain2 = load("gain2", wg2, F32)
 
         h1 = {}
         for b in range(2):
@@ -188,9 +186,7 @@ def tile_list_pallet_pool_features_kernel(
                 nc.scalar.activation(gelu[:, t, :], bank[:], ACT.Gelu_apprx_tanh, scale=slope[:, b, t : t + 1])
                 banks.append(bank)
             if engine != "fused":
-                for t in range(PACK):
-                    nc.scalar.activation(gelu[:, t, :], gelu[:, t, :], ACT.Copy, scale=inverse[:, b, t : t + 1])
-                return quantize_plain("z1_%d_%d" % (c, b), gelu, engine), banks
+                return gelu, banks
             grouped = grouped_tile()
             factor = inverse[:, b, :].unsqueeze(1).unsqueeze(3).to_broadcast([P, CHUNK // 4, PACK, 4])
             nc.vector.tensor_tensor(word_order(grouped), plane_order(gelu), factor, ALU.mult)
@@ -230,7 +226,7 @@ def tile_list_pallet_pool_features_kernel(
         place_depots(0, 1)
         w3_mx = [quantize_dealt("w3_0", w3_raw[0], "scalar")]
         keep_h1(1, 0, banks)
-        z1[(1, 1)], last_banks = depots(1, 1, "vector")
+        last_planes, last_banks = depots(1, 1, "scalar")
 
         w2_dealt = held("w2_dealt", [P, H], U16)
         nc.vector.tensor_copy(
@@ -244,6 +240,8 @@ def tile_list_pallet_pool_features_kernel(
         )
         w5_raw = [load_weight(w5, a, 0) for a in range(2)]
         w6_raw = load_weight(w6, 0, 0)
+        idx4 = load("idx4", offs4, U16)
+        gain2 = load("gain2", wg2, F32)
 
         def reduce_angle(b, t):
             angle = product([(columns(w3_mx[b], t), v2)])
@@ -271,15 +269,18 @@ def tile_list_pallet_pool_features_kernel(
 
         planes = [planes_tile()]
         customers(0, 0, planes[0], 0, 2)
+        for t in range(PACK):
+            nc.scalar.activation(last_planes[:, t, :], last_planes[:, t, :], ACT.Copy, scale=inverse[:, 1, t : t + 1])
         w3_mx.append(quantize_dealt("w3_1", w3_raw[1], "scalar"))
         customers(0, 1, planes[0], 0, 3)
+        z1[(1, 1)] = quantize_plain("z1_1_1", last_planes, "scalar")
         keep_h1(1, 1, last_banks)
-        w5_mx = [quantize_plain("w5_0", w5_raw[0], "scalar")]
         planes.append(planes_tile())
         customers(1, 0, planes[1], 1, 0)
         z2 = [quantize_plain("z2_0", planes[0], "scalar")]
-        w5_mx.append(quantize_plain("w5_1", w5_raw[1], "scalar"))
+        w5_mx = [quantize_plain("w5_0", w5_raw[0], "scalar")]
         customers(1, 1, planes[1], 1, 1)
+        w5_mx.append(quantize_plain("w5_1", w5_raw[1], "scalar"))
         w6_mx = quantize_plain("w6", w6_raw, "scalar")
         place_depots(1, 2)
         z2.append(quantize_plain("z2_1", planes[1], "scalar"))

import math
from contextlib import ExitStack

import concourse.mybir as mybir

K, K2, H, N, T, S, C, T2 = 1024, 512, 1024, 512, 2048, 1024, 512, 2048
FLOPS = 2 * (K * H * S + 2 * K2 * H * C + H * N * S + H * N * C + K2 * N * C)

F32 = mybir.dt.float32
BF16 = mybir.dt.bfloat16
I32 = mybir.dt.int32
U32 = mybir.dt.uint32
U16 = mybir.dt.uint16
U8 = mybir.dt.uint8
FP8X4 = mybir.dt.float8_e4m3fn_x4
FP4X4 = mybir.dt.float4_e2m1fn_x4
ALU = mybir.AluOpType
ACT = mybir.ActivationFunctionType

P = 128
PACK = 4
PASS = P * PACK
CHUNK = 512
LIST_COLS = CHUNK // 16
ROUND_TO_INTEGER = 1.5 * 2.0**23


def tile_list_pallet_pool_features_kernel(
    tc, tab_words, tab_scales, tab2_words, tab2_scales, offs, offs2, pos1, offs3, offs4, w1, r1,
    w2_words, w2_scales, w3, w4_words, w4_scales, w5, w6, page1, wg1, wg2, out,
):
    nc = tc.nc
    with ExitStack() as ctx:
        keep = ctx.enter_context(tc.tile_pool(name="keep", bufs=1))
        ring = ctx.enter_context(tc.tile_pool(name="ring", bufs=2))
        psum = ctx.enter_context(tc.psum_pool(name="psum", bufs=1))

        def held(name, shape, dtype):
            return keep.tile(shape, dtype, name=name, align_bytes=64)

        def load(name, source, dtype):
            tile = held(name, list(source.shape), dtype)
            nc.sync.dma_start(tile[:], source)
            return tile

        def zeroed_plane(name, columns):
            plane = held(name, [P, columns], U8)
            nc.vector.memset(plane[:].bitcast(I32), 0)
            return plane

        def load_words(name, words):
            return load(name, words.rearrange("p t i -> p (t i)").bitcast(I32), I32)

        def load_weight(weight, a, b):
            raw = ring.tile([P, PACK, CHUNK], F32, name="raw", bufs=4)
            rows = weight[a * PASS : (a + 1) * PASS, b * CHUNK : (b + 1) * CHUNK]
            nc.sync.dma_start(raw[:], rows.rearrange("(p j) c -> p j c", j=PACK))
            return raw

        def copy_on(engine, dst, src):
            if engine == "vector":
                nc.vector.tensor_copy(dst, src)
            else:
                nc.scalar.copy(dst, src)

        def grouped_tile():
            return ring.tile([P, CHUNK * PACK], BF16, name="grouped", bufs=3, align_bytes=64)

        def quantize(name, grouped):
            codes = held(name + "_codes", [P, CHUNK], U32)
            scales = held(name + "_scales", [P, CHUNK], U8)
            nc.vector.quantize_mx(out=codes[:].bitcast(FP8X4), scales=scales[:], in_=grouped[:])
            return codes[:].bitcast(FP8X4), scales[:]

        def word_order(grouped):
            return grouped[:].rearrange("p (c i j) -> p c j i", i=4, j=PACK)

        def plane_order(planes):
            return planes[:].rearrange("p j (c i) -> p c j i", i=4)

        def quantize_dealt(name, raw, engine):
            grouped = grouped_tile()
            copy_on(
                engine,
                grouped[:].rearrange("p (t m j) -> p m j t", t=PACK, j=PACK),
                raw[:].rearrange("p j (m t) -> p m j t", t=PACK),
            )
            return quantize(name, grouped)

        def quantize_plain(name, raw, engine):
            grouped = grouped_tile()
            copy_on(engine, word_order(grouped), plane_order(raw))
            return quantize(name, grouped)

        def gather(name, window, offsets, dtype):
            picked = held(name, [P, CHUNK], dtype)
            nc.vector.tensor_copy(picked[:], window[:].bitcast(dtype).indirect(offsets))
            return picked

        def columns(operand, i):
            codes, scales = operand
            return codes[:, i * P : (i + 1) * P], scales[:, i * P : (i + 1) * P]

        def product(passes):
            bank = psum.tile([P, CHUNK], F32, name="bank", bufs=8)
            for i, (stationary, moving) in enumerate(passes):
                nc.tensor.matmul_mx(
                    out=bank[:], lhsT=stationary[0], lhsT_scale=stationary[1], rhs=moving[0], rhs_scale=moving[1],
                    start=(i == 0), stop=(i == len(passes) - 1),
                )
            return bank

        tab_plane = zeroed_plane("tab_plane", T)
        tab2_plane = zeroed_plane("tab2_plane", T)
        w4_plane = zeroed_plane("w4_plane", 2 * N)
        w2_plane = zeroed_plane("w2_plane", H)

        def load_page(n):
            return load("page_%d" % n, page1[n * P : (n + 1) * P, :], F32)

        w1_raw, pages = {}, []
        idx = load("idx", offs, U16)
        tab = [load_words("tab_0", tab_words[0])]
        for q in range(4):
            nc.sync.dma_start(tab_plane[32 * q : 32 * q + 8, :].bitcast(I32), tab_scales[:, 4 * q : 4 * q + 4, :].bitcast(I32))
        w1_raw[(0, 0)] = load_weight(w1, 0, 0)
        tab.append(load_words("tab_1", tab_words[1]))
        w1_raw[(1, 0)] = load_weight(w1, 1, 0)
        w1_raw[(0, 1)] = load_weight(w1, 0, 1)
        w2_raw = load("w2_raw", w2_words[0].bitcast(I32), I32)
        for q in range(4):
            nc.sync.dma_start(w2_plane[32 * q : 32 * q + 4, :].bitcast(I32), w2_scales[0, 4 * q : 4 * q + 4, :].bitcast(I32))
        w1_raw[(1, 1)] = load_weight(w1, 1, 1)
        slope = load("slope", r1.rearrange("(b p t) -> p b t", p=P, t=PACK), F32)
        idx2 = load("idx2", offs2, U16)
        tab2 = load_words("tab2", tab2_words[0])
        for q in range(4):
            nc.sync.dma_start(tab2_plane[32 * q : 32 * q + 4, :].bitcast(I32), tab2_scales[0, 4 * q : 4 * q + 4, :].bitcast(I32))
        w3_raw = [load_weight(w3, 0, 0)]
        w4_codes = load("w4_codes", w4_words.rearrange("a p c -> p a c").bitcast(I32), I32)
        for q in range(4):
            nc.sync.dma_start(
                w4_plane[32 * q : 32 * q + 4, :].bitcast(I32).rearrange("r (a c) -> r a c", a=2),
                w4_scales[:, 4 * q : 4 * q + 4, :].bitcast(I32).rearrange("a r c -> r a c"),
            )
        idx3 = load("idx3", offs3, U16)
        gain1 = load("gain1", wg1, F32)
        pages.append(load_page(0))
        pages.append(load_page(1))
        home = load("home", pos1, U16)
        pages.append(load_page(2))

        def chunk_offsets(offsets, c):
            return offsets[:, c * LIST_COLS : (c + 1) * LIST_COLS]

        v_words, v_plane, w1_mx = {}, {}, {}
        for c in range(2):
            v_words[(0, c)] = gather("v_0_%d" % c, tab[0], chunk_offsets(idx, c), U32)
            v_plane[c] = gather("v_plane_%d" % c, tab_plane, chunk_offsets(idx, c), U8)
        w1_mx[(0, 0)] = quantize_dealt("w1_0_0", w1_raw[(0, 0)], "scalar")
        for c in range(2):
            v_words[(1, c)] = gather("v_1_%d" % c, tab[1], chunk_offsets(idx, c), U32)
        v = [[(v_words[(a, c)][:].bitcast(FP8X4), v_plane[c][4 * a :, :]) for a in range(2)] for c in range(2)]
        w1_mx[(1, 0)] = quantize_dealt("w1_1_0", w1_raw[(1, 0)], "vector")
        inverse = held("inverse", [P, 2, PACK], F32)
        nc.vector.reciprocal(inverse[:], slope[:])
        for a in range(2):
            w1_mx[(a, 1)] = quantize_dealt("w1_%d_1" % a, w1_raw[(a, 1)], "vector")

        w3_raw.append(load_weight(w3, 0, 1))
        pages.append(load_page(3))

        h1 = {}
        for b in range(2):
            for t in range(PACK):
                h1[(b, t)] = held("h1_%d_%d" % (b, t), [P, S], F32)

        def planes_tile():
            return ring.tile([P, PACK, CHUNK], F32, name="planes", bufs=2)

        def depots(c, b, engine="fused"):
            gelu = planes_tile()
            banks = []
            for t in range(PACK):
                bank = product([(columns(w1_mx[(a, b)], t), v[c][a]) for a in range(2)])
                nc.scalar.activation(gelu[:, t, :], bank[:], ACT.Gelu_apprx_tanh, scale=slope[:, b, t : t + 1])
                banks.append(bank)
            if engine != "fused":
                return gelu, banks
            grouped = grouped_tile()
            factor = inverse[:, b, :].unsqueeze(1).unsqueeze(3).to_broadcast([P, CHUNK // 4, PACK, 4])
            nc.vector.tensor_tensor(word_order(grouped), plane_order(gelu), factor, ALU.mult)
            return quantize("z1_%d_%d" % (c, b), grouped), banks

        def keep_h1(c, b, banks):
            for t in range(PACK):
                nc.scalar.copy(h1[(b, t)][:, c * CHUNK : (c + 1) * CHUNK], banks[t][:])

        def place(n, passes, offsets, gain):
            bank = product(passes)
            y = ring.tile([P, CHUNK], F32, name="y", bufs=3)
            nc.scalar.copy(y[:], bank[:])
            nc.vector.tensor_tensor(pages[n][:].indirect(offsets), y[:], gain, ALU.mult)

        w4_bytes = w4_codes[:].bitcast(U8)

        def w4_columns(b, n):
            codes = w4_bytes[:, b, 2 * n * P : 2 * (n + 1) * P].bitcast(FP4X4)
            return codes, w4_plane[:, b * N + n * P : b * N + (n + 1) * P]

        z1 = {}

        def place_depots(c, n):
            passes = [(w4_columns(b, n), z1[(c, b)]) for b in range(2)]
            place(n, passes, chunk_offsets(idx3, c), gain1[:, c * CHUNK : (c + 1) * CHUNK])

        for b in range(2):
            z1[(0, b)], banks = depots(0, b)
            keep_h1(0, b, banks)
        v2_words = gather("v2", tab2, idx2[:], U32)
        v2_plane = gather("v2_plane", tab2_plane, idx2[:], U8)
        v2 = (v2_words[:].bitcast(FP8X4), v2_plane[:])

        z1[(1, 0)], banks = depots(1, 0)
        place_depots(0, 0)
        place_depots(0, 1)
        w3_mx = [quantize_dealt("w3_0", w3_raw[0], "scalar")]
        keep_h1(1, 0, banks)
        last_planes, last_banks = depots(1, 1, "scalar")

        w2_dealt = held("w2_dealt", [P, H], U16)
        nc.vector.tensor_copy(
            w2_dealt[:].rearrange("p (b t m) -> p b m t", b=2, t=PACK),
            w2_raw[:].bitcast(U16).rearrange("p (b m t) -> p b m t", b=2, t=PACK),
        )
        w2_dealt_plane = held("w2_dealt_plane", [P, H], U8)
        nc.vector.tensor_copy(
            w2_dealt_plane[:].rearrange("p (b t m) -> p b m t", b=2, t=PACK),
            w2_plane[:].rearrange("p (b m t) -> p b m t", b=2, t=PACK),
        )
        w5_raw = [load_weight(w5, a, 0) for a in range(2)]
        w6_raw = load_weight(w6, 0, 0)
        idx4 = load("idx4", offs4, U16)
        gain2 = load("gain2", wg2, F32)

        def reduce_angle(b, t):
            angle = product([(columns(w3_mx[b], t), v2)])
            shifted = ring.tile([P, CHUNK], U32, name="shifted", bufs=2)
            nc.scalar.activation(shifted[:], angle[:], ACT.Copy, bias=ROUND_TO_INTEGER, scale=1.0 / (2.0 * math.pi))
            h2 = ring.tile([P, CHUNK], F32, name="h2", bufs=4)
            nc.scalar.activation(h2[:], shifted[:], ACT.Copy, bias=-ROUND_TO_INTEGER, scale=1.0)
            nc.vector.scalar_tensor_tensor(h2[:], h2[:], -2.0 * math.pi, angle[:], ALU.mult, ALU.add)
            return h2

        def meet_depot(b, t, h2, planes):
            i = b * PACK + t
            nc.scalar.activation(h2[:], h2[:], ACT.Sin)
            w2_columns = (w2_dealt[:, i * P : (i + 1) * P].bitcast(FP4X4), w2_dealt_plane[:, i * P : (i + 1) * P])
            linear = product([(w2_columns, v2)])
            nc.vector.tensor_tensor(h2[:], linear[:], h2[:], ALU.add)
            nc.vector.tensor_tensor(planes[:, t, :], h1[(b, t)][:].indirect(home[:]), h2[:], ALU.mult)

        def customers(b, pair, planes, c, n):
            slots = (2 * pair, 2 * pair + 1)
            angles = [reduce_angle(b, t) for t in slots]
            place_depots(c, n)
            for t, h2 in zip(slots, angles):
                meet_depot(b, t, h2, planes)

        planes = [planes_tile()]
        customers(0, 0, planes[0], 0, 2)
        for t in range(PACK):
            nc.scalar.activation(last_planes[:, t, :], last_planes[:, t, :], ACT.Copy, scale=inverse[:, 1, t : t + 1])
        w3_mx.append(quantize_dealt("w3_1", w3_raw[1], "scalar"))
        customers(0, 1, planes[0], 0, 3)
        z1[(1, 1)] = quantize_plain("z1_1_1", last_planes, "scalar")
        keep_h1(1, 1, last_banks)
        planes.append(planes_tile())
        customers(1, 0, planes[1], 1, 0)
        z2 = [quantize_plain("z2_0", planes[0], "scalar")]
        w5_mx = [quantize_plain("w5_0", w5_raw[0], "scalar")]
        customers(1, 1, planes[1], 1, 1)
        w5_mx.append(quantize_plain("w5_1", w5_raw[1], "scalar"))
        w6_mx = quantize_plain("w6", w6_raw, "scalar")
        place_depots(1, 2)
        z2.append(quantize_plain("z2_1", planes[1], "scalar"))
        place_depots(1, 3)

        for n in range(N // P):
            passes = [(columns(w6_mx, n), v2)] + [(columns(w5_mx[b], n), z2[b]) for b in range(2)]
            place(n, passes, idx4[:], gain2[:])
            nc.sync.dma_start(out[n * P : (n + 1) * P, :], pages[n][:])
